import numpy as np
import ml_dtypes


def mxq(x, axis, fmt="e4m3"):
    dtype, down = {"e4m3": (ml_dtypes.float8_e4m3fn, 7), "e5m2": (ml_dtypes.float8_e5m2, 14)}[fmt]
    v = np.moveaxis(np.asarray(x, np.float32).astype(ml_dtypes.bfloat16).astype(np.float64), axis, -1)
    blocks = v.reshape(v.shape[:-1] + (-1, 32))
    amax = np.abs(blocks).max(-1, keepdims=True)
    byte = np.maximum(np.where(amax > 0, np.frexp(amax)[1] - 1 + 127, 0) - down, 1)
    scale = np.exp2(byte - 127.0)
    codes = (blocks / scale).astype(np.float32).astype(dtype).astype(np.float64)
    return np.moveaxis((codes * scale).reshape(v.shape), -1, axis)


WIDE = False


def mx_kscale(k):
    if not WIDE:
        return np.ones(k)
    levels = np.array([10, -10, 5, -5, 0])
    if k % 512:
        return np.exp2(np.random.permutation(np.resize(levels, k // 32))).repeat(32)
    a = np.empty((k // 512, 16))
    for p in range(k // 512):
        a[p, :8] = np.random.permutation(np.resize(levels, 8))
        for g in range(8):
            far = levels[np.abs(levels - a[p, g]) >= 10]
            a[p, g + 8] = far[np.random.randint(len(far))]
    return np.exp2(a.ravel()).repeat(32)


def f64(x):
    return np.asarray(x).astype(np.float64)


def striped(idx):
    return np.tile(np.asarray(idx).reshape(-1, 16).T, (8, 1)).astype(np.uint16)


def unstriped(offs):
    return offs[:16].T.reshape(-1).astype(np.int64)


E2M1 = np.array([0.0, 0.5, 1.0, 1.5, 2.0, 3.0, 4.0, 6.0, -0.0, -0.5, -1.0, -1.5, -2.0, -3.0, -4.0, -6.0])


def pack_weight(w, fmt):
    k, n = w.shape
    w = f64(np.asarray(w, np.float32).astype(ml_dtypes.bfloat16)).reshape(k // 32, 32, n)
    amax = np.abs(w).max(1)
    if fmt == "e4m3":
        byte = np.frexp(amax)[1] - 1 + 127 - 7
    else:
        mant, ex = np.frexp(amax / 6.0)
        byte = np.where(mant > 0.5, ex, ex - 1) + 127
    byte = np.clip(np.where(amax > 0, byte, 1), 1, 254)
    scaled = (w * np.exp2(127.0 - byte)[:, None, :]).reshape(k, n).astype(np.float32)
    by_word = np.ascontiguousarray(scaled.reshape(k // 512, 128, 4, n).transpose(0, 1, 3, 2))
    if fmt == "e4m3":
        words = by_word.astype(ml_dtypes.float8_e4m3fn).view(np.uint8)
    else:
        c = by_word.astype(ml_dtypes.float4_e2m1fn).view(np.uint8) & 0xF
        words = (c[..., 0::2] | (c[..., 1::2] << 4)).reshape(k // 512, 128, 2 * n)
    return np.ascontiguousarray(words), np.ascontiguousarray(byte.astype(np.uint8).reshape(k // 512, 16, n))


def unpack_weight(words, scales, fmt):
    g, _, n = scales.shape
    words = np.ascontiguousarray(words).reshape(g, 128, n, -1)
    if fmt == "e4m3":
        vals = words.view(ml_dtypes.float8_e4m3fn).astype(np.float64)
    else:
        nib = np.empty((g, 128, n, 4), np.uint8)
        nib[..., 0::2] = words & 0xF
        nib[..., 1::2] = words >> 4
        vals = E2M1[nib]
    vals = vals * np.repeat(np.exp2(scales.astype(np.float64) - 127.0), 8, axis=1)[..., None]
    return vals.transpose(0, 1, 3, 2).reshape(g * 512, n)


B, N, T, D, DV, NQ = 1, 512, 1024, 512, 256, 256


def setup_inputs():
    n = np.random.standard_normal
    idx = np.sort(np.random.permutation(T)[:B * N].reshape(B, N), axis=1).reshape(-1)
    s = mx_kscale(D)[:, None]
    u = np.ones(T)
    u[idx] = mx_kscale(B * N)
    r = np.random.uniform(0.5, 2.0, T)
    qp = [pack_weight(x, "e4m3") for x in n((B, D, NQ)) * s * (0.80 / np.sqrt(D))]
    k = n((D, T)) / s
    v = n((DV, T)) / (u * r)
    kp = pack_weight(k, "e4m3")
    return {
        "q_words": np.stack([x[0] for x in qp]),
        "q_scales": np.stack([x[1] for x in qp]),
        "k_words": kp[0],
        "k_scales": kp[1],
        "vT": v.astype(np.float32),
        "vs": np.tile(u * r, (128, 1)).astype(np.float32),
        "kb": np.tile(n(T), (128, 1)).astype(np.float32),
        "og": n((B, NQ, DV)).astype(np.float32),
        "offs": striped(idx),
    }


def reference(q_words, q_scales, k_words, k_scales, vT, vs, kb, og, offs):
    idx = unstriped(offs)
    k = unpack_weight(k_words, k_scales, "e4m3")
    v = f64(vT)
    pick = lambda x: x[:, idx].reshape(x.shape[0], B, N).transpose(1, 0, 2)
    q = np.stack([unpack_weight(q_words[b], q_scales[b], "e4m3") for b in range(B)])
    score = q.transpose(0, 2, 1) @ pick(k)
    score = score + pick(f64(kb))[:, :1, :]
    m = score.max(-1, keepdims=True)
    p = np.exp(score - m)
    total = p.sum(-1, keepdims=True)
    w = p * pick(f64(vs))[:, :1, :]
    y = mxq(w, 2, "e4m3") @ mxq(pick(v).transpose(0, 2, 1), 1, "e4m3")
    y = y / total
    y = y / (1.0 + np.exp(-f64(og)))
    return y

@@ -1,0 +1,205 @@
+from contextlib import ExitStack
+
+import concourse.mybir as mybir
+from concourse.masks import make_identity
+
+F32 = mybir.dt.float32
+BF16 = mybir.dt.bfloat16
+I32 = mybir.dt.int32
+U32 = mybir.dt.uint32
+U16 = mybir.dt.uint16
+U8 = mybir.dt.uint8
+FP8X4 = mybir.dt.float8_e4m3fn_x4
+ACT = mybir.ActivationFunctionType
+ALU = mybir.AluOpType
+
+P = 128
+PACK = 4
+SLOTS = 512
+TOKENS = 1024
+FEATURES = 512
+VALUE_FEATURES = 256
+QUERIES = 256
+Q_TILES = QUERIES // P
+FLOPS = 2 * QUERIES * SLOTS * (FEATURES + VALUE_FEATURES)
+
+
+def tile_attend_soft_kb_gate_srtq256n512t1024_kernel(tc, q_words, q_scales, k_words, k_scales, vT, vs, kb, og, offs, out):
+    nc = tc.nc
+    with ExitStack() as ctx:
+        keep = ctx.enter_context(tc.tile_pool(name="keep", bufs=1))
+        psum = ctx.enter_context(tc.psum_pool(name="psum", bufs=1))
+
+        offsets = keep.tile([P, SLOTS // 16], U16, name="offsets")
+        nc.sync.dma_start(offsets[:], offs)
+
+        key_scales = keep.tile([P, TOKENS], U8, name="key_scales")
+        nc.gpsimd.memset(key_scales[:].bitcast(I32), 0)
+        key_scale_rows = k_scales[0].bitcast(I32).rearrange("(g r) c -> r g c", r=PACK)
+        for r in range(PACK):
+            nc.scalar.dma_start(key_scales[r:P:32, :].bitcast(I32), key_scale_rows[r])
+
+        key_words = keep.tile([P, TOKENS], U32, name="key_words", tag="pool_a")
+        nc.sync.dma_start(key_words[:].bitcast(I32), k_words[0].rearrange("p t r -> p (t r)").bitcast(I32))
+
+        values_lo = keep.tile([P, TOKENS], F32, name="values_lo", tag="pool_b")
+        nc.sync.dma_start(values_lo[:], vT[0:P, :])
+
+        query_words = keep.tile([P, QUERIES], U32, name="query_words", align_bytes=64)
+        nc.sync.dma_start(query_words[:].bitcast(I32), q_words[0, 0].rearrange("p q r -> p (q r)").bitcast(I32))
+
+        bias_pool = keep.tile([P, TOKENS], F32, name="bias_pool")
+        nc.vector.memset(bias_pool[:], 0.0)
+        nc.scalar.dma_start(bias_pool[0:1, :], kb[0:1, :])
+
+        query_scales = keep.tile([P, QUERIES], U8, name="query_scales", align_bytes=64)
+        nc.gpsimd.memset(query_scales[:].bitcast(I32), 0)
+        query_scale_rows = q_scales[0, 0].bitcast(I32).rearrange("(g r) c -> r g c", r=PACK)
+        for r in range(PACK):
+            nc.sync.dma_start(query_scales[r:P:32, :].bitcast(I32), query_scale_rows[r])
+
+        scale_pool = keep.tile([P, TOKENS], F32, name="scale_pool")
+        nc.vector.memset(scale_pool[:], 0.0)
+        nc.sync.dma_start(scale_pool[0:1, :], vs[0:1, :])
+
+        identity = keep.tile([P, P], F32, name="identity")
+        make_identity(nc, identity[:])
+
+        keys = keep.tile([P, SLOTS], U32, name="keys", align_bytes=64)
+        nc.vector.tensor_copy(keys[:], key_words[:].indirect(offsets[:]))
+        keys_scale = keep.tile([P, SLOTS], U8, name="keys_scale", align_bytes=64)
+        nc.vector.tensor_copy(keys_scale[:], key_scales[:].indirect(offsets[:]))
+        bias_row = keep.tile([P, SLOTS], F32, name="bias_row")
+        nc.vector.tensor_copy(bias_row[:], bias_pool[:].indirect(offsets[:]))
+        scale_row = keep.tile([P, SLOTS], F32, name="scale_row")
+        nc.vector.tensor_copy(scale_row[:], scale_pool[:].indirect(offsets[:]))
+
+        values_hi = keep.tile([P, TOKENS], F32, name="values_hi", tag="pool_a")
+        nc.sync.dma_start(values_hi[:], vT[P : 2 * P, :])
+
+        raw = []
+        for h in range(Q_TILES):
+            raw_bank = psum.tile([P, PACK, P], F32, name=f"raw_bank{h}", tag=f"bank_a{h}")
+            q_cols = slice(h * P, (h + 1) * P)
+            for j in range(PACK):
+                k_cols = slice(j * P, (j + 1) * P)
+                nc.tensor.matmul_mx(
+                    out=raw_bank[:, j, :],
+                    lhsT=keys[:, k_cols].bitcast(FP8X4),
+                    lhsT_scale=keys_scale[:, k_cols],
+                    rhs=query_words[:, q_cols].bitcast(FP8X4),
+                    rhs_scale=query_scales[:, q_cols],
+                    start=True,
+                    stop=True,
+                )
+            raw_h = keep.tile([P, PACK, P], F32, name=f"raw{h}")
+            nc.scalar.copy(raw_h[:], raw_bank[:])
+            raw.append(raw_h)
+
+        bias_bank = psum.tile([P, PACK, P], F32, name="bias_bank", tag="bank_c0")
+        for j in range(PACK):
+            nc.tensor.transpose(bias_bank[:, j, :], bias_row[:, j * P : (j + 1) * P], identity[:])
+        bias_col = keep.tile([P, PACK], F32, name="bias_col")
+        nc.scalar.copy(bias_col[:], bias_bank[:, :, 0])
+
+        values_lo_bf = keep.tile([P, TOKENS], BF16, name="values_lo_bf")
+        nc.scalar.activation(values_lo_bf[:], values_lo[:], ACT.Copy)
+        picked_lo = keep.tile([P, SLOTS], BF16, name="picked_lo")
+        nc.scalar.activation(picked_lo[:], values_lo_bf[:].indirect(offsets[:]), ACT.Copy)
+
+        gate_in = keep.tile([P, Q_TILES, VALUE_FEATURES], F32, name="gate_in", tag="pool_b")
+        nc.sync.dma_start(gate_in[:], og[0].rearrange("(h p) e -> p h e", p=P))
+
+        scale_bank = psum.tile([P, PACK, P], F32, name="scale_bank", tag="bank_c1")
+        for t in range(PACK):
+            nc.tensor.transpose(scale_bank[:, t, :], scale_row[:, t:SLOTS:PACK], identity[:])
+        scale_col = keep.tile([P, PACK], F32, name="scale_col")
+        nc.scalar.copy(scale_col[:], scale_bank[:, :, 0])
+
+        score_banks = []
+        for h in range(Q_TILES):
+            score_bank = psum.tile([P, SLOTS], F32, name=f"score_bank{h}", tag=f"bank_s{h}")
+            for j in range(PACK):
+                nc.tensor.matmul(score_bank[:, j * P : (j + 1) * P], raw[h][:, j, :], identity[:],
+                                 start=(j == 0), stop=False, is_transpose=True)
+            for j in range(PACK):
+                nc.tensor.matmul(score_bank[:, j * P : (j + 1) * P], bias_col[:, j : j + 1].to_broadcast([P, P]), identity[:],
+                                 start=False, stop=(j == PACK - 1), is_transpose=True)
+            score_banks.append(score_bank)
+
+        neg_max = []
+        for h in range(Q_TILES):
+            neg_max_h = keep.tile([P, 1], F32, name=f"neg_max{h}")
+            nc.vector.tensor_reduce(neg_max_h[:], score_banks[h][:], mybir.AxisListType.X, ALU.max, negate=True)
+            neg_max.append(neg_max_h)
+
+        picked_hi = keep.tile([P, SLOTS], BF16, name="picked_hi")
+        nc.vector.tensor_copy(picked_hi[:], values_hi[:].indirect(offsets[:]))
+
+        total = keep.tile([P, Q_TILES], F32, name="total")
+        prob_banks = []
+        for h in range(Q_TILES):
+            prob = keep.tile([P, PACK, P], F32, name=f"prob{h}")
+            nc.scalar.activation(prob[:], score_banks[h][:].rearrange("q (s t) -> q t s", t=PACK), ACT.Exp,
+                                 bias=neg_max[h][:], accum_out=total[:, h : h + 1])
+            prob_bank = psum.tile([P, PACK, P], F32, name=f"prob_bank{h}", tag=f"bank_a{h}")
+            for t in range(PACK):
+                nc.tensor.transpose(prob_bank[:, t, :], prob[:, t, :], identity[:])
+            prob_banks.append(prob_bank)
+
+        value_codes = keep.tile([P, VALUE_FEATURES], U32, name="value_codes", align_bytes=64)
+        value_scales = keep.tile([P, VALUE_FEATURES], U8, name="value_scales", align_bytes=64)
+        value_groups = keep.tile([P, VALUE_FEATURES * PACK], BF16, name="value_groups", align_bytes=64)
+        for b, picked in enumerate((picked_lo, picked_hi)):
+            pairs = picked[:].bitcast(F32)
+            value_bank = psum.tile([P, 2, P], F32, name=f"value_bank{b}", tag=f"bank_v{b}")
+            for u in range(2):
+                nc.tensor.transpose(value_bank[:, u, :], pairs[:, u : SLOTS // 2 : 2], identity[:])
+            nc.scalar.copy(
+                value_groups[:, b * SLOTS : (b + 1) * SLOTS].bitcast(F32).rearrange("s (e u) -> s e u", u=2),
+                value_bank[:].rearrange("s u e -> s e u"),
+            )
+
+        gate_tanh = keep.tile([P, Q_TILES * VALUE_FEATURES], F32, name="gate_tanh")
+        nc.scalar.activation(gate_tanh[:], gate_in[:].rearrange("p h e -> p (h e)"), ACT.Tanh, scale=0.5)
+        gate = keep.tile([P, Q_TILES * VALUE_FEATURES], F32, name="gate")
+        nc.gpsimd.tensor_scalar(gate[:], gate_tanh[:], 0.5, 0.5, ALU.mult, ALU.add)
+
+        weights = []
+        for h in range(Q_TILES):
+            weight = keep.tile([P, P, PACK], BF16, name=f"weight{h}", align_bytes=64)
+            nc.vector.tensor_tensor(
+                weight[:],
+                prob_banks[h][:].rearrange("s t q -> s q t"),
+                scale_col[:].unsqueeze(1).to_broadcast([P, P, PACK]),
+                ALU.mult,
+            )
+            weights.append(weight)
+
+        nc.vector.quantize_mx(out=value_codes[:].bitcast(FP8X4), scales=value_scales[:], in_=value_groups[:])
+        inverse = keep.tile([P, Q_TILES], F32, name="inverse")
+        nc.vector.reciprocal(inverse[:], total[:])
+
+        sums = []
+        for h in range(Q_TILES):
+            weight_codes = keep.tile([P, P], U32, name=f"weight_codes{h}", align_bytes=64)
+            weight_scales = keep.tile([P, P], U8, name=f"weight_scales{h}", align_bytes=64)
+            nc.vector.quantize_mx(out=weight_codes[:].bitcast(FP8X4), scales=weight_scales[:],
+                                  in_=weights[h][:].rearrange("s q t -> s (q t)"))
+            sum_bank = psum.tile([P, VALUE_FEATURES], F32, name=f"sum_bank{h}", tag=f"bank_c{h}")
+            nc.tensor.matmul_mx(
+                out=sum_bank[:],
+                lhsT=weight_codes[:].bitcast(FP8X4),
+                lhsT_scale=weight_scales[:],
+                rhs=value_codes[:].bitcast(FP8X4),
+                rhs_scale=value_scales[:],
+                start=True,
+                stop=True,
+            )
+            sums.append(sum_bank)
+
+        for h in range(Q_TILES):
+            result = keep.tile([P, VALUE_FEATURES], F32, name=f"result{h}")
+            nc.vector.scalar_tensor_tensor(result[:], sums[h][:], inverse[:, h : h + 1],
+                                           gate[:, h * VALUE_FEATURES : (h + 1) * VALUE_FEATURES], ALU.mult, ALU.mult)
+            nc.sync.dma_start(out[0, h * P : (h + 1) * P, :], result[:])

@@ -21,7 +21,17 @@ FEATURES = 512
 VALUE_FEATURES = 256
 QUERIES = 256
 Q_TILES = QUERIES // P
+HALF = SLOTS // 2
+ROW0 = 96
 FLOPS = 2 * QUERIES * SLOTS * (FEATURES + VALUE_FEATURES)
+
+
+def load_scale_rows(nc, plane, rows):
+    words = rows.bitcast(I32)
+    width = words.shape[1]
+    for g in range(PACK):
+        quad = words[PACK * g : PACK * (g + 1), :].unsqueeze(0).to_broadcast([8, PACK, width])
+        nc.sync.dma_start(plane[32 * g : 32 * (g + 1), :].bitcast(I32), quad)
 
 
 def tile_attend_soft_kb_gate_srtq256n512t1024_kernel(tc, q_words, q_scales, k_words, k_scales, vT, vs, kb, og, offs, out):
@@ -33,108 +43,102 @@ def tile_attend_soft_kb_gate_srtq256n512t1024_kernel(tc, q_words, q_scales, k_wo
         offsets = keep.tile([P, SLOTS // 16], U16, name="offsets")
         nc.sync.dma_start(offsets[:], offs)
 
-        key_scales = keep.tile([P, TOKENS], U8, name="key_scales")
-        nc.gpsimd.memset(key_scales[:].bitcast(I32), 0)
-        key_scale_rows = k_scales[0].bitcast(I32).rearrange("(g r) c -> r g c", r=PACK)
-        for r in range(PACK):
-            nc.scalar.dma_start(key_scales[r:P:32, :].bitcast(I32), key_scale_rows[r])
+        bias_pool = keep.tile([P, TOKENS], F32, name="bias_pool", tag="buf_kb")
+        nc.sync.dma_start(bias_pool[ROW0:P, :], kb[ROW0:P, :])
+        nc.vector.memset(bias_pool[0:ROW0, :], 0.0)
 
-        key_words = keep.tile([P, TOKENS], U32, name="key_words", tag="pool_a")
+        key_scales = keep.tile([P, TOKENS], U8, name="key_scales", tag="buf_ks")
+        load_scale_rows(nc, key_scales, k_scales[0])
+        key_words = keep.tile([P, TOKENS], U32, name="key_words", tag="buf_kw")
         nc.sync.dma_start(key_words[:].bitcast(I32), k_words[0].rearrange("p t r -> p (t r)").bitcast(I32))
-
-        values_lo = keep.tile([P, TOKENS], F32, name="values_lo", tag="pool_b")
-        nc.sync.dma_start(values_lo[:], vT[0:P, :])
 
         query_words = keep.tile([P, QUERIES], U32, name="query_words", align_bytes=64)
         nc.sync.dma_start(query_words[:].bitcast(I32), q_words[0, 0].rearrange("p q r -> p (q r)").bitcast(I32))
-
-        bias_pool = keep.tile([P, TOKENS], F32, name="bias_pool")
-        nc.vector.memset(bias_pool[:], 0.0)
-        nc.scalar.dma_start(bias_pool[0:1, :], kb[0:1, :])
-
         query_scales = keep.tile([P, QUERIES], U8, name="query_scales", align_bytes=64)
-        nc.gpsimd.memset(query_scales[:].bitcast(I32), 0)
-        query_scale_rows = q_scales[0, 0].bitcast(I32).rearrange("(g r) c -> r g c", r=PACK)
-        for r in range(PACK):
-            nc.sync.dma_start(query_scales[r:P:32, :].bitcast(I32), query_scale_rows[r])
+        load_scale_rows(nc, query_scales, q_scales[0, 0])
 
-        scale_pool = keep.tile([P, TOKENS], F32, name="scale_pool")
-        nc.vector.memset(scale_pool[:], 0.0)
-        nc.sync.dma_start(scale_pool[0:1, :], vs[0:1, :])
+        scale_pool = keep.tile([P, TOKENS], F32, name="scale_pool", tag="buf_vs")
+        nc.sync.dma_start(scale_pool[ROW0:P, :], vs[ROW0:P, :])
+        nc.vector.memset(scale_pool[0:ROW0, :], 0.0)
+
+        values_lo = keep.tile([P, TOKENS], F32, name="values_lo")
+        nc.sync.dma_start(values_lo[:], vT[0:P, :])
+        values_hi = keep.tile([P, TOKENS], F32, name="values_hi")
+        nc.sync.dma_start(values_hi[:], vT[P : 2 * P, :])
+        gate_in = keep.tile([P, Q_TILES, VALUE_FEATURES], F32, name="gate_in")
+        nc.sync.dma_start(gate_in[:], og[0].rearrange("(h p) e -> p h e", p=P))
 
         identity = keep.tile([P, P], F32, name="identity")
         make_identity(nc, identity[:])
 
-        keys = keep.tile([P, SLOTS], U32, name="keys", align_bytes=64)
-        nc.vector.tensor_copy(keys[:], key_words[:].indirect(offsets[:]))
-        keys_scale = keep.tile([P, SLOTS], U8, name="keys_scale", align_bytes=64)
-        nc.vector.tensor_copy(keys_scale[:], key_scales[:].indirect(offsets[:]))
         bias_row = keep.tile([P, SLOTS], F32, name="bias_row")
         nc.vector.tensor_copy(bias_row[:], bias_pool[:].indirect(offsets[:]))
-        scale_row = keep.tile([P, SLOTS], F32, name="scale_row")
+        keys_scale = keep.tile([P, SLOTS], U8, name="keys_scale", align_bytes=64)
+        nc.vector.tensor_copy(keys_scale[:], key_scales[:].indirect(offsets[:]))
+        keys = keep.tile([P, SLOTS], U32, name="keys", align_bytes=64)
+        for half in range(2):
+            nc.vector.tensor_copy(keys[:, half * HALF : (half + 1) * HALF],
+                                  key_words[:].indirect(offsets[:, half * HALF // 16 : (half + 1) * HALF // 16]))
+        scale_row = keep.tile([P, SLOTS], F32, name="scale_row", tag="buf_kw")
         nc.vector.tensor_copy(scale_row[:], scale_pool[:].indirect(offsets[:]))
-
-        values_hi = keep.tile([P, TOKENS], F32, name="values_hi", tag="pool_a")
-        nc.sync.dma_start(values_hi[:], vT[P : 2 * P, :])
-
-        raw = []
-        for h in range(Q_TILES):
-            raw_bank = psum.tile([P, PACK, P], F32, name=f"raw_bank{h}", tag=f"bank_a{h}")
-            q_cols = slice(h * P, (h + 1) * P)
-            for j in range(PACK):
-                k_cols = slice(j * P, (j + 1) * P)
-                nc.tensor.matmul_mx(
-                    out=raw_bank[:, j, :],
-                    lhsT=keys[:, k_cols].bitcast(FP8X4),
-                    lhsT_scale=keys_scale[:, k_cols],
-                    rhs=query_words[:, q_cols].bitcast(FP8X4),
-                    rhs_scale=query_scales[:, q_cols],
-                    start=True,
-                    stop=True,
-                )
-            raw_h = keep.tile([P, PACK, P], F32, name=f"raw{h}")
-            nc.scalar.copy(raw_h[:], raw_bank[:])
-            raw.append(raw_h)
+        picked_lo = keep.tile([P, SLOTS], BF16, name="picked_lo", tag="buf_vs")
+        nc.vector.tensor_copy(picked_lo[:], values_lo[:].indirect(offsets[:]))
 
         bias_bank = psum.tile([P, PACK, P], F32, name="bias_bank", tag="bank_c0")
         for j in range(PACK):
             nc.tensor.transpose(bias_bank[:, j, :], bias_row[:, j * P : (j + 1) * P], identity[:])
         bias_col = keep.tile([P, PACK], F32, name="bias_col")
-        nc.scalar.copy(bias_col[:], bias_bank[:, :, 0])
-
-        values_lo_bf = keep.tile([P, TOKENS], BF16, name="values_lo_bf")
-        nc.scalar.activation(values_lo_bf[:], values_lo[:], ACT.Copy)
-        picked_lo = keep.tile([P, SLOTS], BF16, name="picked_lo")
-        nc.scalar.activation(picked_lo[:], values_lo_bf[:].indirect(offsets[:]), ACT.Copy)
-
-        gate_in = keep.tile([P, Q_TILES, VALUE_FEATURES], F32, name="gate_in", tag="pool_b")
-        nc.sync.dma_start(gate_in[:], og[0].rearrange("(h p) e -> p h e", p=P))
-
-        scale_bank = psum.tile([P, PACK, P], F32, name="scale_bank", tag="bank_c1")
-        for t in range(PACK):
-            nc.tensor.transpose(scale_bank[:, t, :], scale_row[:, t:SLOTS:PACK], identity[:])
-        scale_col = keep.tile([P, PACK], F32, name="scale_col")
-        nc.scalar.copy(scale_col[:], scale_bank[:, :, 0])
+        nc.scalar.copy(bias_col[:], bias_bank[:, :, ROW0])
 
         score_banks = []
         for h in range(Q_TILES):
             score_bank = psum.tile([P, SLOTS], F32, name=f"score_bank{h}", tag=f"bank_s{h}")
             for j in range(PACK):
-                nc.tensor.matmul(score_bank[:, j * P : (j + 1) * P], raw[h][:, j, :], identity[:],
-                                 start=(j == 0), stop=False, is_transpose=True)
-            for j in range(PACK):
                 nc.tensor.matmul(score_bank[:, j * P : (j + 1) * P], bias_col[:, j : j + 1].to_broadcast([P, P]), identity[:],
-                                 start=False, stop=(j == PACK - 1), is_transpose=True)
+                                 start=(j == 0), stop=False, is_transpose=True)
             score_banks.append(score_bank)
+
+        def raw_scores(bank, j, q_cols):
+            k_cols = slice(j * P, (j + 1) * P)
+            nc.tensor.matmul_mx(
+                out=bank,
+                lhsT=keys[:, k_cols].bitcast(FP8X4),
+                lhsT_scale=keys_scale[:, k_cols],
+                rhs=query_words[:, q_cols].bitcast(FP8X4),
+                rhs_scale=query_scales[:, q_cols],
+                start=True,
+                stop=True,
+            )
+
+        early_bank = psum.tile([P, 2, QUERIES], F32, name="early_bank", tag="bank_r0")
+        for j in range(2):
+            raw_scores(early_bank[:, j, :], j, slice(0, QUERIES))
+        early = keep.tile([P, 2, QUERIES], F32, name="early", tag="buf_early")
+        nc.scalar.copy(early[:], early_bank[:])
+        late = []
+        for h in range(Q_TILES):
+            late_bank = psum.tile([P, 2, P], F32, name=f"late_bank{h}", tag=f"bank_r{h + 1}")
+            for j in range(2):
+                raw_scores(late_bank[:, j, :], 2 + j, slice(h * P, (h + 1) * P))
+            late_h = keep.tile([P, 2, P], F32, name=f"late{h}")
+            nc.scalar.copy(late_h[:], late_bank[:])
+            late.append(late_h)
+
+        for h in range(Q_TILES):
+            for j in range(PACK):
+                raw = early[:, j, h * P : (h + 1) * P] if j < 2 else late[h][:, j - 2, :]
+                nc.tensor.matmul(score_banks[h][:, j * P : (j + 1) * P], raw, identity[:],
+                                 start=False, stop=(j == PACK - 1), is_transpose=True)
+
+        scale_bank = psum.tile([P, PACK, P], F32, name="scale_bank", tag="bank_r2")
+        for t in range(PACK):
+            nc.tensor.transpose(scale_bank[:, t, :], scale_row[:, t:SLOTS:PACK], identity[:])
 
         neg_max = []
         for h in range(Q_TILES):
-            neg_max_h = keep.tile([P, 1], F32, name=f"neg_max{h}")
+            neg_max_h = keep.tile([P, 1], F32, name=f"neg_max{h}", tag=f"buf_max{h}")
             nc.vector.tensor_reduce(neg_max_h[:], score_banks[h][:], mybir.AxisListType.X, ALU.max, negate=True)
             neg_max.append(neg_max_h)
-
-        picked_hi = keep.tile([P, SLOTS], BF16, name="picked_hi")
-        nc.vector.tensor_copy(picked_hi[:], values_hi[:].indirect(offsets[:]))
 
         total = keep.tile([P, Q_TILES], F32, name="total")
         prob_banks = []
@@ -142,17 +146,23 @@ def tile_attend_soft_kb_gate_srtq256n512t1024_kernel(tc, q_words, q_scales, k_wo
             prob = keep.tile([P, PACK, P], F32, name=f"prob{h}")
             nc.scalar.activation(prob[:], score_banks[h][:].rearrange("q (s t) -> q t s", t=PACK), ACT.Exp,
                                  bias=neg_max[h][:], accum_out=total[:, h : h + 1])
-            prob_bank = psum.tile([P, PACK, P], F32, name=f"prob_bank{h}", tag=f"bank_a{h}")
+            prob_bank = psum.tile([P, PACK, P], F32, name=f"prob_bank{h}", tag=f"bank_r{h}")
             for t in range(PACK):
                 nc.tensor.transpose(prob_bank[:, t, :], prob[:, t, :], identity[:])
             prob_banks.append(prob_bank)
+
+        scale_col = keep.tile([P, PACK], F32, name="scale_col")
+        nc.scalar.copy(scale_col[:], scale_bank[:, :, ROW0])
+
+        picked_hi = keep.tile([P, SLOTS], BF16, name="picked_hi", tag="buf_max0")
+        nc.vector.tensor_copy(picked_hi[:], values_hi[:].indirect(offsets[:]))
 
         value_codes = keep.tile([P, VALUE_FEATURES], U32, name="value_codes", align_bytes=64)
         value_scales = keep.tile([P, VALUE_FEATURES], U8, name="value_scales", align_bytes=64)
         value_groups = keep.tile([P, VALUE_FEATURES * PACK], BF16, name="value_groups", align_bytes=64)
         for b, picked in enumerate((picked_lo, picked_hi)):
             pairs = picked[:].bitcast(F32)
-            value_bank = psum.tile([P, 2, P], F32, name=f"value_bank{b}", tag=f"bank_v{b}")
+            value_bank = psum.tile([P, 2, P], F32, name=f"value_bank{b}", tag=f"bank_s{b}")
             for u in range(2):
                 nc.tensor.transpose(value_bank[:, u, :], pairs[:, u : SLOTS // 2 : 2], identity[:])
             nc.scalar.copy(
@@ -160,7 +170,7 @@ def tile_attend_soft_kb_gate_srtq256n512t1024_kernel(tc, q_words, q_scales, k_wo
                 value_bank[:].rearrange("s u e -> s e u"),
             )
 
-        gate_tanh = keep.tile([P, Q_TILES * VALUE_FEATURES], F32, name="gate_tanh")
+        gate_tanh = keep.tile([P, Q_TILES * VALUE_FEATURES], F32, name="gate_tanh", tag="buf_early")
         nc.scalar.activation(gate_tanh[:], gate_in[:].rearrange("p h e -> p (h e)"), ACT.Tanh, scale=0.5)
         gate = keep.tile([P, Q_TILES * VALUE_FEATURES], F32, name="gate")
         nc.gpsimd.tensor_scalar(gate[:], gate_tanh[:], 0.5, 0.5, ALU.mult, ALU.add)

@@ -81,6 +81,7 @@ def tile_attend_soft_kb_gate_srtq256n512t1024_kernel(tc, q_words, q_scales, k_wo
                                   key_words[:].indirect(offsets[:, half * HALF // 16 : (half + 1) * HALF // 16]))
         scale_row = keep.tile([P, SLOTS], F32, name="scale_row", tag="buf_kw")
         nc.vector.tensor_copy(scale_row[:], scale_pool[:].indirect(offsets[:]))
+
         picked_lo = keep.tile([P, SLOTS], BF16, name="picked_lo", tag="buf_vs")
         nc.vector.tensor_copy(picked_lo[:], values_lo[:].indirect(offsets[:]))
 
@@ -89,14 +90,6 @@ def tile_attend_soft_kb_gate_srtq256n512t1024_kernel(tc, q_words, q_scales, k_wo
             nc.tensor.transpose(bias_bank[:, j, :], bias_row[:, j * P : (j + 1) * P], identity[:])
         bias_col = keep.tile([P, PACK], F32, name="bias_col")
         nc.scalar.copy(bias_col[:], bias_bank[:, :, ROW0])
-
-        score_banks = []
-        for h in range(Q_TILES):
-            score_bank = psum.tile([P, SLOTS], F32, name=f"score_bank{h}", tag=f"bank_s{h}")
-            for j in range(PACK):
-                nc.tensor.matmul(score_bank[:, j * P : (j + 1) * P], bias_col[:, j : j + 1].to_broadcast([P, P]), identity[:],
-                                 start=(j == 0), stop=False, is_transpose=True)
-            score_banks.append(score_bank)
 
         def raw_scores(bank, j, q_cols):
             k_cols = slice(j * P, (j + 1) * P)
@@ -113,22 +106,35 @@ def tile_attend_soft_kb_gate_srtq256n512t1024_kernel(tc, q_words, q_scales, k_wo
         early_bank = psum.tile([P, 2, QUERIES], F32, name="early_bank", tag="bank_r0")
         for j in range(2):
             raw_scores(early_bank[:, j, :], j, slice(0, QUERIES))
-        early = keep.tile([P, 2, QUERIES], F32, name="early", tag="buf_early")
-        nc.scalar.copy(early[:], early_bank[:])
-        late = []
+        score_banks = []
         for h in range(Q_TILES):
             late_bank = psum.tile([P, 2, P], F32, name=f"late_bank{h}", tag=f"bank_r{h + 1}")
             for j in range(2):
                 raw_scores(late_bank[:, j, :], 2 + j, slice(h * P, (h + 1) * P))
-            late_h = keep.tile([P, 2, P], F32, name=f"late{h}")
-            nc.scalar.copy(late_h[:], late_bank[:])
-            late.append(late_h)
-
-        for h in range(Q_TILES):
+            score_bank = psum.tile([P, SLOTS], F32, name=f"score_bank{h}", tag=f"bank_s{h}")
             for j in range(PACK):
-                raw = early[:, j, h * P : (h + 1) * P] if j < 2 else late[h][:, j - 2, :]
-                nc.tensor.matmul(score_banks[h][:, j * P : (j + 1) * P], raw, identity[:],
-                                 start=False, stop=(j == PACK - 1), is_transpose=True)
+                raw = early_bank[:, j, h * P : (h + 1) * P] if j < 2 else late_bank[:, j - 2, :]
+                biased = keep.tile([P, P], F32, name=f"biased{h}{j}")
+                nc.scalar.activation(biased[:], raw, ACT.Identity, bias=bias_col[:, j : j + 1])
+                nc.tensor.transpose(score_bank[:, j * P : (j + 1) * P], biased[:], identity[:])
+            score_banks.append(score_bank)
+
+        value_codes = keep.tile([P, VALUE_FEATURES], U32, name="value_codes", align_bytes=64)
+        value_scales = keep.tile([P, VALUE_FEATURES], U8, name="value_scales", align_bytes=64)
+        value_groups = []
+
+        def turn_values(b, picked, bank_tag):
+            pairs = picked[:].bitcast(F32)
+            value_bank = psum.tile([P, 2, P], F32, name=f"value_bank{b}", tag=bank_tag)
+            for u in range(2):
+                nc.tensor.transpose(value_bank[:, u, :], pairs[:, u : SLOTS // 2 : 2], identity[:])
+            group = keep.tile([P, P * PACK], BF16, name=f"value_group{b}", align_bytes=64)
+            nc.scalar.copy(group[:].bitcast(F32).rearrange("s (e u) -> s e u", u=2), value_bank[:].rearrange("s u e -> s e u"))
+            value_groups.append(group)
+
+        def quantize_values(b):
+            e_cols = slice(b * P, (b + 1) * P)
+            nc.vector.quantize_mx(out=value_codes[:, e_cols].bitcast(FP8X4), scales=value_scales[:, e_cols], in_=value_groups[b][:])
 
         scale_bank = psum.tile([P, PACK, P], F32, name="scale_bank", tag="bank_r2")
         for t in range(PACK):
@@ -157,23 +163,15 @@ def tile_attend_soft_kb_gate_srtq256n512t1024_kernel(tc, q_words, q_scales, k_wo
         picked_hi = keep.tile([P, SLOTS], BF16, name="picked_hi", tag="buf_max0")
         nc.vector.tensor_copy(picked_hi[:], values_hi[:].indirect(offsets[:]))
 
-        value_codes = keep.tile([P, VALUE_FEATURES], U32, name="value_codes", align_bytes=64)
-        value_scales = keep.tile([P, VALUE_FEATURES], U8, name="value_scales", align_bytes=64)
-        value_groups = keep.tile([P, VALUE_FEATURES * PACK], BF16, name="value_groups", align_bytes=64)
-        for b, picked in enumerate((picked_lo, picked_hi)):
-            pairs = picked[:].bitcast(F32)
-            value_bank = psum.tile([P, 2, P], F32, name=f"value_bank{b}", tag=f"bank_s{b}")
-            for u in range(2):
-                nc.tensor.transpose(value_bank[:, u, :], pairs[:, u : SLOTS // 2 : 2], identity[:])
-            nc.scalar.copy(
-                value_groups[:, b * SLOTS : (b + 1) * SLOTS].bitcast(F32).rearrange("s (e u) -> s e u", u=2),
-                value_bank[:].rearrange("s u e -> s e u"),
-            )
+        turn_values(0, picked_lo, "bank_s0")
+        turn_values(1, picked_hi, "bank_s1")
 
-        gate_tanh = keep.tile([P, Q_TILES * VALUE_FEATURES], F32, name="gate_tanh", tag="buf_early")
+        gate_tanh = keep.tile([P, Q_TILES * VALUE_FEATURES], F32, name="gate_tanh", tag="buf_max1")
         nc.scalar.activation(gate_tanh[:], gate_in[:].rearrange("p h e -> p (h e)"), ACT.Tanh, scale=0.5)
         gate = keep.tile([P, Q_TILES * VALUE_FEATURES], F32, name="gate")
         nc.gpsimd.tensor_scalar(gate[:], gate_tanh[:], 0.5, 0.5, ALU.mult, ALU.add)
+
+        quantize_values(0)
 
         weights = []
         for h in range(Q_TILES):
@@ -186,9 +184,6 @@ def tile_attend_soft_kb_gate_srtq256n512t1024_kernel(tc, q_words, q_scales, k_wo
             )
             weights.append(weight)
 
-        nc.vector.quantize_mx(out=value_codes[:].bitcast(FP8X4), scales=value_scales[:], in_=value_groups[:])
-        inverse = keep.tile([P, Q_TILES], F32, name="inverse")
-        nc.vector.reciprocal(inverse[:], total[:])
 
         sums = []
         for h in range(Q_TILES):
@@ -196,6 +191,8 @@ def tile_attend_soft_kb_gate_srtq256n512t1024_kernel(tc, q_words, q_scales, k_wo
             weight_scales = keep.tile([P, P], U8, name=f"weight_scales{h}", align_bytes=64)
             nc.vector.quantize_mx(out=weight_codes[:].bitcast(FP8X4), scales=weight_scales[:],
                                   in_=weights[h][:].rearrange("s q t -> s (q t)"))
+            if h == 0:
+                quantize_values(1)
             sum_bank = psum.tile([P, VALUE_FEATURES], F32, name=f"sum_bank{h}", tag=f"bank_c{h}")
             nc.tensor.matmul_mx(
                 out=sum_bank[:],
@@ -208,6 +205,8 @@ def tile_attend_soft_kb_gate_srtq256n512t1024_kernel(tc, q_words, q_scales, k_wo
             )
             sums.append(sum_bank)
 
+        inverse = keep.tile([P, Q_TILES], F32, name="inverse")
+        nc.vector.reciprocal(inverse[:], total[:])
         for h in range(Q_TILES):
             result = keep.tile([P, VALUE_FEATURES], F32, name=f"result{h}")
             nc.vector.scalar_tensor_tensor(result[:], sums[h][:], inverse[:, h : h + 1],

from contextlib import ExitStack

import concourse.mybir as mybir
from concourse.masks import make_identity

F32 = mybir.dt.float32
BF16 = mybir.dt.bfloat16
I32 = mybir.dt.int32
U32 = mybir.dt.uint32
U16 = mybir.dt.uint16
U8 = mybir.dt.uint8
FP8X4 = mybir.dt.float8_e4m3fn_x4
ACT = mybir.ActivationFunctionType
ALU = mybir.AluOpType

P = 128
PACK = 4
SLOTS = 512
TOKENS = 1024
FEATURES = 512
VALUE_FEATURES = 256
QUERIES = 256
Q_TILES = QUERIES // P
HALF = SLOTS // 2
ROW0 = 96
FLOPS = 2 * QUERIES * SLOTS * (FEATURES + VALUE_FEATURES)


def load_scale_rows(nc, plane, rows):
    words = rows.bitcast(I32)
    width = words.shape[1]
    for g in range(PACK):
        quad = words[PACK * g : PACK * (g + 1), :].unsqueeze(0).to_broadcast([8, PACK, width])
        nc.sync.dma_start(plane[32 * g : 32 * (g + 1), :].bitcast(I32), quad)


def tile_attend_soft_kb_gate_srtq256n512t1024_kernel(tc, q_words, q_scales, k_words, k_scales, vT, vs, kb, og, offs, out):
    nc = tc.nc
    with ExitStack() as ctx:
        keep = ctx.enter_context(tc.tile_pool(name="keep", bufs=1))
        psum = ctx.enter_context(tc.psum_pool(name="psum", bufs=1))

        offsets = keep.tile([P, SLOTS // 16], U16, name="offsets")
        nc.sync.dma_start(offsets[:], offs)

        bias_pool = keep.tile([P, TOKENS], F32, name="bias_pool", tag="buf_kb")
        nc.sync.dma_start(bias_pool[ROW0:P, :], kb[ROW0:P, :])
        nc.vector.memset(bias_pool[0:ROW0, :], 0.0)

        key_scales = keep.tile([P, TOKENS], U8, name="key_scales", tag="buf_ks")
        load_scale_rows(nc, key_scales, k_scales[0])
        key_words = keep.tile([P, TOKENS], U32, name="key_words", tag="buf_kw")
        nc.sync.dma_start(key_words[:].bitcast(I32), k_words[0].rearrange("p t r -> p (t r)").bitcast(I32))

        query_words = keep.tile([P, QUERIES], U32, name="query_words", align_bytes=64)
        nc.sync.dma_start(query_words[:].bitcast(I32), q_words[0, 0].rearrange("p q r -> p (q r)").bitcast(I32))
        query_scales = keep.tile([P, QUERIES], U8, name="query_scales", align_bytes=64)
        load_scale_rows(nc, query_scales, q_scales[0, 0])

        scale_pool = keep.tile([P, TOKENS], F32, name="scale_pool", tag="buf_vs")
        nc.sync.dma_start(scale_pool[ROW0:P, :], vs[ROW0:P, :])
        nc.vector.memset(scale_pool[0:ROW0, :], 0.0)

        values_lo = keep.tile([P, TOKENS], F32, name="values_lo")
        nc.sync.dma_start(values_lo[:], vT[0:P, :])
        values_hi = keep.tile([P, TOKENS], F32, name="values_hi")
        nc.sync.dma_start(values_hi[:], vT[P : 2 * P, :])
        gate_in = keep.tile([P, Q_TILES, VALUE_FEATURES], F32, name="gate_in")
        nc.sync.dma_start(gate_in[:], og[0].rearrange("(h p) e -> p h e", p=P))

        identity = keep.tile([P, P], F32, name="identity")
        make_identity(nc, identity[:])

        bias_row = keep.tile([P, SLOTS], F32, name="bias_row")
        nc.vector.tensor_copy(bias_row[:], bias_pool[:].indirect(offsets[:]))
        keys_scale = keep.tile([P, SLOTS], U8, name="keys_scale", align_bytes=64)
        nc.vector.tensor_copy(keys_scale[:], key_scales[:].indirect(offsets[:]))
        keys = keep.tile([P, SLOTS], U32, name="keys", align_bytes=64)
        for half in range(2):
            nc.vector.tensor_copy(keys[:, half * HALF : (half + 1) * HALF],
                                  key_words[:].indirect(offsets[:, half * HALF // 16 : (half + 1) * HALF // 16]))
        scale_row = keep.tile([P, SLOTS], F32, name="scale_row", tag="buf_kw")
        nc.vector.tensor_copy(scale_row[:], scale_pool[:].indirect(offsets[:]))

        picked_lo = keep.tile([P, SLOTS], BF16, name="picked_lo", tag="buf_vs")
        nc.vector.tensor_copy(picked_lo[:], values_lo[:].indirect(offsets[:]))

        bias_bank = psum.tile([P, PACK, P], F32, name="bias_bank", tag="bank_c0")
        for j in range(PACK):
            nc.tensor.transpose(bias_bank[:, j, :], bias_row[:, j * P : (j + 1) * P], identity[:])
        bias_col = keep.tile([P, PACK], F32, name="bias_col")
        nc.scalar.copy(bias_col[:], bias_bank[:, :, ROW0])

        def raw_scores(bank, j, q_cols):
            k_cols = slice(j * P, (j + 1) * P)
            nc.tensor.matmul_mx(
                out=bank,
                lhsT=keys[:, k_cols].bitcast(FP8X4),
                lhsT_scale=keys_scale[:, k_cols],
                rhs=query_words[:, q_cols].bitcast(FP8X4),
                rhs_scale=query_scales[:, q_cols],
                start=True,
                stop=True,
            )

        early_bank = psum.tile([P, 2, QUERIES], F32, name="early_bank", tag="bank_r0")
        for j in range(2):
            raw_scores(early_bank[:, j, :], j, slice(0, QUERIES))
        score_banks = []
        for h in range(Q_TILES):
            late_bank = psum.tile([P, 2, P], F32, name=f"late_bank{h}", tag=f"bank_r{h + 1}")
            for j in range(2):
                raw_scores(late_bank[:, j, :], 2 + j, slice(h * P, (h + 1) * P))
            score_bank = psum.tile([P, SLOTS], F32, name=f"score_bank{h}", tag=f"bank_s{h}")
            for j in range(PACK):
                raw = early_bank[:, j, h * P : (h + 1) * P] if j < 2 else late_bank[:, j - 2, :]
                biased = keep.tile([P, P], F32, name=f"biased{h}{j}")
                nc.scalar.activation(biased[:], raw, ACT.Identity, bias=bias_col[:, j : j + 1])
                nc.tensor.transpose(score_bank[:, j * P : (j + 1) * P], biased[:], identity[:])
            score_banks.append(score_bank)

        value_codes = keep.tile([P, VALUE_FEATURES], U32, name="value_codes", align_bytes=64)
        value_scales = keep.tile([P, VALUE_FEATURES], U8, name="value_scales", align_bytes=64)
        value_groups = []

        def turn_values(b, picked, bank_tag):
            pairs = picked[:].bitcast(F32)
            value_bank = psum.tile([P, 2, P], F32, name=f"value_bank{b}", tag=bank_tag)
            for u in range(2):
                nc.tensor.transpose(value_bank[:, u, :], pairs[:, u : SLOTS // 2 : 2], identity[:])
            group = keep.tile([P, P * PACK], BF16, name=f"value_group{b}", align_bytes=64)
            nc.scalar.copy(group[:].bitcast(F32).rearrange("s (e u) -> s e u", u=2), value_bank[:].rearrange("s u e -> s e u"))
            value_groups.append(group)

        def quantize_values(b):
            e_cols = slice(b * P, (b + 1) * P)
            nc.vector.quantize_mx(out=value_codes[:, e_cols].bitcast(FP8X4), scales=value_scales[:, e_cols], in_=value_groups[b][:])

        scale_bank = psum.tile([P, PACK, P], F32, name="scale_bank", tag="bank_r2")
        for t in range(PACK):
            nc.tensor.transpose(scale_bank[:, t, :], scale_row[:, t:SLOTS:PACK], identity[:])

        neg_max = []
        for h in range(Q_TILES):
            neg_max_h = keep.tile([P, 1], F32, name=f"neg_max{h}", tag=f"buf_max{h}")
            nc.vector.tensor_reduce(neg_max_h[:], score_banks[h][:], mybir.AxisListType.X, ALU.max, negate=True)
            neg_max.append(neg_max_h)

        total = keep.tile([P, Q_TILES], F32, name="total")
        prob_banks = []
        for h in range(Q_TILES):
            prob = keep.tile([P, PACK, P], F32, name=f"prob{h}")
            nc.scalar.activation(prob[:], score_banks[h][:].rearrange("q (s t) -> q t s", t=PACK), ACT.Exp,
                                 bias=neg_max[h][:], accum_out=total[:, h : h + 1])
            prob_bank = psum.tile([P, PACK, P], F32, name=f"prob_bank{h}", tag=f"bank_r{h}")
            for t in range(PACK):
                nc.tensor.transpose(prob_bank[:, t, :], prob[:, t, :], identity[:])
            prob_banks.append(prob_bank)

        scale_col = keep.tile([P, PACK], F32, name="scale_col")
        nc.scalar.copy(scale_col[:], scale_bank[:, :, ROW0])

        picked_hi = keep.tile([P, SLOTS], BF16, name="picked_hi", tag="buf_max0")
        nc.vector.tensor_copy(picked_hi[:], values_hi[:].indirect(offsets[:]))

        turn_values(0, picked_lo, "bank_s0")
        turn_values(1, picked_hi, "bank_s1")

        gate_tanh = keep.tile([P, Q_TILES * VALUE_FEATURES], F32, name="gate_tanh", tag="buf_max1")
        nc.scalar.activation(gate_tanh[:], gate_in[:].rearrange("p h e -> p (h e)"), ACT.Tanh, scale=0.5)
        gate = keep.tile([P, Q_TILES * VALUE_FEATURES], F32, name="gate")
        nc.gpsimd.tensor_scalar(gate[:], gate_tanh[:], 0.5, 0.5, ALU.mult, ALU.add)

        quantize_values(0)

        weights = []
        for h in range(Q_TILES):
            weight = keep.tile([P, P, PACK], BF16, name=f"weight{h}", align_bytes=64)
            nc.vector.tensor_tensor(
                weight[:],
                prob_banks[h][:].rearrange("s t q -> s q t"),
                scale_col[:].unsqueeze(1).to_broadcast([P, P, PACK]),
                ALU.mult,
            )
            weights.append(weight)


        sums = []
        for h in range(Q_TILES):
            weight_codes = keep.tile([P, P], U32, name=f"weight_codes{h}", align_bytes=64)
            weight_scales = keep.tile([P, P], U8, name=f"weight_scales{h}", align_bytes=64)
            nc.vector.quantize_mx(out=weight_codes[:].bitcast(FP8X4), scales=weight_scales[:],
                                  in_=weights[h][:].rearrange("s q t -> s (q t)"))
            if h == 0:
                quantize_values(1)
            sum_bank = psum.tile([P, VALUE_FEATURES], F32, name=f"sum_bank{h}", tag=f"bank_c{h}")
            nc.tensor.matmul_mx(
                out=sum_bank[:],
                lhsT=weight_codes[:].bitcast(FP8X4),
                lhsT_scale=weight_scales[:],
                rhs=value_codes[:].bitcast(FP8X4),
                rhs_scale=value_scales[:],
                start=True,
                stop=True,
            )
            sums.append(sum_bank)

        inverse = keep.tile([P, Q_TILES], F32, name="inverse")
        nc.vector.reciprocal(inverse[:], total[:])
        for h in range(Q_TILES):
            result = keep.tile([P, VALUE_FEATURES], F32, name=f"result{h}")
            nc.vector.scalar_tensor_tensor(result[:], sums[h][:], inverse[:, h : h + 1],
                                           gate[:, h * VALUE_FEATURES : (h + 1) * VALUE_FEATURES], ALU.mult, ALU.mult)
            nc.sync.dma_start(out[0, h * P : (h + 1) * P, :], result[:])
